import numpy as np
CORES = [36,164,52,180,100,228,116,244]
N = 8
TK = 512
D = 128 * N
EPS = 0.01
def setup_inputs(rng):
    x = rng.standard_normal((N, 128, TK), dtype=np.float32) * (0.5 + np.abs(rng.standard_normal((1, 1, TK), dtype=np.float32))) + rng.standard_normal((1, 1, TK), dtype=np.float32)
    return {"x": x, "dy": rng.standard_normal((N, 128, TK), dtype=np.float32) + 0.5 * x + rng.standard_normal((1, 1, TK), dtype=np.float32)}
def setup_inputs_big(rng):
    d = setup_inputs(rng)
    for k in ("x", "dy"): d[k] = (d[k].astype(np.float32) * 1024.0).astype(d[k].dtype)
    return d
def setup_inputs_small(rng):
    d = setup_inputs(rng)
    for k in ("x", "dy"): d[k] = (d[k].astype(np.float32) * (1 / 1024.0)).astype(d[k].dtype)
    return d
def setup_inputs_apart(rng):
    d = setup_inputs(rng)
    f = (10.0 ** rng.permutation(np.linspace(-1.5, 1.5, N))).astype(np.float32).reshape(N, 1, 1)
    for k in ("x",): d[k] = (d[k].astype(np.float32) * f).astype(d[k].dtype)
    return d
def setup_inputs_mixed(rng):
    d = setup_inputs(rng)
    f = (10.0 ** rng.uniform(-3, 3, (1, 1, TK))).astype(np.float32); shape = rng.integers(3, size=(1, 1, TK))
    for k in ("x", "dy"):
        x = d[k].astype(np.float32)
        m = x.mean(axis=(0, 1), keepdims=True); level = m + np.sign(x - m) * np.abs(x - m).mean(axis=(0, 1), keepdims=True) * rng.uniform(0.9, 1.1, x.shape).astype(np.float32)
        other = x * np.where(rng.random(x.shape) < 0.5, 0.1, 1.0).astype(np.float32)
        d[k] = (np.where(shape == 1, level, np.where(shape == 2, other, x)) * f).astype(d[k].dtype)
    return d
def setup_inputs_offset(rng):
    d = setup_inputs(rng)
    x = d["x"]; spread = x.std(axis=(0, 1), keepdims=True)
    d["x"] = (x + spread * rng.uniform(16, 48, (1, 1, TK)) * rng.choice([-1.0, 1.0], (1, 1, TK))).astype(np.float32)
    return d
def reference(x, dy):
    X, DY = x.astype(np.float64), dy.astype(np.float64)
    mu = X.sum(axis=(0, 1)) / D
    rs = 1.0 / np.sqrt(((X - mu) ** 2).sum(axis=(0, 1)) / D + EPS)
    n = (X - mu) * rs
    a = DY.sum(axis=(0, 1)) / D; c = (DY * n).sum(axis=(0, 1)) / D
    return {"dx": (rs * (DY - a - n * c)).astype(np.float32)}

@@ -1,0 +1,203 @@
+from concourse.bass import DstId, RemoteDMATransfer
+from concourse.mybir import AluOpType, AxisListType, ActivationFunctionType
+
+NR = 8
+NCH = 4
+W = 5 * NCH
+NEV = 120
+
+SCRATCH = {
+    "xs": ("sbuf", [128, 512], "float32"),
+    "ds": ("sbuf", [128, 512], "float32"),
+    "pm": ("sbuf", [128, 132], "float32"),
+    "idn": ("sbuf", [128, 128], "float32"),
+    "xc": ("sbuf", [128, 512], "float32"),
+    "junk": ("sbuf", [128, 512], "float32"),
+    "prod": ("sbuf", [128, 512], "float32"),
+    "ub": ("sbuf", [128, 512], "float32"),
+    "vb": ("sbuf", [128, 512], "float32"),
+    "dg": ("sbuf", [128, 512], "float32"),
+    "ob": ("sbuf", [128, 512], "float32"),
+    "G": ("sbuf", [128, NR, W], "float32"),
+    "S1": ("sbuf", [128, 4, W], "float32"),
+    "S2": ("sbuf", [128, 2, W], "float32"),
+    "S3": ("sbuf", [128, 3 * NCH], "float32"),
+    "DD": ("sbuf", [128, 7, 3 * NCH], "float32"),
+    "DW": ("sbuf", [128, 7, 2 * NCH], "float32"),
+    "Q8": ("sbuf", [128, 8, 2 * NCH], "float32"),
+    "R4": ("sbuf", [128, 4, 2 * NCH], "float32"),
+    "R2": ("sbuf", [128, 2, 2 * NCH], "float32"),
+    "TOT": ("sbuf", [128, 2 * NCH], "float32"),
+    "OD": ("sbuf", [128, 2 * NCH], "float32"),
+    "sd": ("sbuf", [128, NCH], "float32"),
+    "rs": ("sbuf", [128, NCH], "float32"),
+    "rs2": ("sbuf", [128, NCH], "float32"),
+    "cv": ("sbuf", [128, NCH], "float32"),
+    "be": ("sbuf", [128, NCH], "float32"),
+}
+for _j in range(NCH):
+    SCRATCH["px%d" % _j] = ("psum", [128, 512], "float32")
+    SCRATCH["pd%d" % _j] = ("psum", [128, 512], "float32")
+
+SEMAPHORES = ["e%d" % _i for _i in range(NEV)] + ["arr", "sent"]
+
+ADD, SUB, MUL = AluOpType.add, AluOpType.subtract, AluOpType.mult
+ACT = ActivationFunctionType
+
+
+def _low_bits(mask, n):
+    out, b = 0, 1
+    while n > 0 and b <= mask:
+        if mask & b:
+            out |= b
+            n -= 1
+        b <<= 1
+    return out
+
+
+def rank_program(g, core, T, topo):
+    r = T.rank_of(core)
+    if r is None:
+        return
+    n = NCH
+    V, S, PE, SY = g.vector, g.scalar, g.tensor, g.sync
+    evs = []
+    seen = {}
+
+    def mark(ins, k=1):
+        e = [T.sem["e%d" % len(evs)], k, len(evs), False]
+        evs.append(e)
+        ins.then_inc(e[0], k)
+        return e
+
+    def wait(q, qn, *es):
+        for e in es:
+            if (qn, e[2]) in seen:
+                continue
+            seen[(qn, e[2])] = True
+            e[3] = True
+            q.wait_ge(e[0], e[1])
+
+    def wv(*es): wait(V, "v", *es)
+    def ws(*es): wait(S, "s", *es)
+    def wp(*es): wait(PE, "p", *es)
+    def wg(*es): wait(g, "g", *es)
+    def wy(*es): wait(SY, "y", *es)
+
+    def ch(t, j):
+        return t[:, 128 * j:128 * (j + 1)]
+
+    lx0 = mark(SY.dma_start(T.xs[0:64, :], T.x[0:64, :]), 16)
+    lx1 = mark(S.dma_start(T.xs[64:128, :], T.x[64:128, :]), 16)
+    ld0 = mark(SY.dma_start(T.ds[0:64, :], T.dy[0:64, :]), 16)
+    ld1 = mark(S.dma_start(T.ds[64:128, :], T.dy[64:128, :]), 16)
+
+    c0 = mark(V.memset(T.pm[:, 0:128], -1.0 / 128))
+    c1 = mark(V.memset(T.pm[:, 128:132], 1.0 / 128))
+    c2 = mark(V.memset(T.idn[:], 0.0))
+    wg(c0)
+    cp = mark(g.affine_select(T.pm[:, 0:128], T.pm[:, 0:128], [[-1, 128]], AluOpType.not_equal, 127.0 / 128, 0, 1))
+    wg(c2)
+    ci = mark(g.affine_select(T.idn[:], T.idn[:], [[-1, 128]], AluOpType.not_equal, 1.0, 0, 1))
+
+    px = [T["px%d" % j] for j in range(n)]
+    pd = [T["pd%d" % j] for j in range(n)]
+    own = []
+
+    wp(cp, c1, lx0, lx1)
+    ex = [mark(PE.matmul(px[j][:, 0:130], ch(T.xs, j), T.pm[:, 0:130], True, True)) for j in range(n)]
+    wp(ld0, ld1)
+    ed = [mark(PE.matmul(pd[j][:, 0:129], ch(T.ds, j), T.pm[:, 0:129], True, True)) for j in range(n)]
+
+    exc = []
+    for j in range(n):
+        ws(ex[j])
+        exc.append(mark(S.activation(ch(T.xc, j), px[j][:, 0:128], ACT.Copy)))
+        own.append(mark(S.activation(ch(T.junk, j), px[j][:, 0:128], ACT.Square,
+                                     accum_out=T.G[:, r, 3 * n + j:3 * n + j + 1])))
+        own.append(mark(S.activation(T.G[:, r, j:j + n + 1:n], px[j][:, 128:130], ACT.Copy)))
+
+    for j in range(n):
+        wv(ed[j], exc[j])
+        ep = mark(V.tensor_tensor(ch(T.prod, j), pd[j][:, 0:128], ch(T.xc, j), MUL))
+        own.append(mark(V.tensor_copy(T.G[:, r, 2 * n + j:2 * n + j + 1], pd[j][:, 128:129])))
+        wv(ep)
+        own.append(mark(V.tensor_reduce(T.G[:, r, 4 * n + j:4 * n + j + 1], ch(T.prod, j), AxisListType.X, ADD)))
+
+    dsts = [T.cores[(r + k) % NR] for k in range(1, NR)]
+    m = topo.mask(core, dsts[0])
+    for d in dsts:
+        m &= topo.mask(core, d)
+    m = _low_bits(m, 8)
+    ne = bin(m).count("1")
+    ids = []
+    for d in dsts:
+        rid, pid = topo.addr(d, core)
+        ids.append(DstId(rid=rid, pnc=pid))
+    wg(*own)
+    g.remote_dma_fused([RemoteDMATransfer(dst_ids=ids, dma_engine_mask=m, remote_sem=T.sem.arr,
+                                          srcs=[T.G[:, r, :]], dsts=[T.G[:, r, :] for _ in dsts], alu_op=0)],
+                       local_sem=T.sem.sent)
+
+    wv(*own)
+    V.wait_ge(T.sem.arr, 7 * ne)
+    G, S1, S2, S3, DD, DW, Q8 = T.G, T.S1, T.S2, T.S3, T.DD, T.DW, T.Q8
+    e_s1 = mark(V.tensor_tensor(S1[:, :, :], G[:, 0:4, :], G[:, 4:8, :], ADD))
+    e_d1 = mark(V.tensor_tensor(DD[:, 0:4, :], G[:, 0:4, 0:3 * n], G[:, 4:8, 0:3 * n], SUB))
+    wv(e_s1)
+    e_s2 = mark(V.tensor_tensor(S2[:, :, :], S1[:, 0:2, :], S1[:, 2:4, :], ADD))
+    e_d2 = mark(V.tensor_tensor(DD[:, 4:6, :], S1[:, 0:2, 0:3 * n], S1[:, 2:4, 0:3 * n], SUB))
+    wv(e_s2)
+    e_d3 = mark(V.tensor_tensor(DD[:, 6, :], S2[:, 0, 0:3 * n], S2[:, 1, 0:3 * n], SUB))
+    e_s3 = mark(V.tensor_tensor(S3[:], S2[:, 0, 0:3 * n], S2[:, 1, 0:3 * n], ADD))
+    e_q7 = mark(V.tensor_tensor(Q8[:, 7, :], S2[:, 0, 3 * n:5 * n], S2[:, 1, 3 * n:5 * n], ADD))
+    ws(e_d1)
+    e_w1 = mark(S.activation(DW[:, 0:4, :], DD[:, 0:4, 0:2 * n], ACT.Copy, scale=64.0))
+    ws(e_d2)
+    e_w2 = mark(S.activation(DW[:, 4:6, :], DD[:, 4:6, 0:2 * n], ACT.Copy, scale=32.0))
+    ws(e_d3)
+    e_w3 = mark(S.activation(DW[:, 6, :], DD[:, 6, 0:2 * n], ACT.Copy, scale=16.0))
+    wv(e_d1, e_d2, e_d3, e_w1, e_w2, e_w3)
+    e_q = mark(V.tensor_tensor(Q8[:, 0:7, :], DW[:, :, :], DD[:, :, n:3 * n], MUL))
+    wv(e_q, e_q7)
+    e_r4 = mark(V.tensor_tensor(T.R4[:, :, :], Q8[:, 0:4, :], Q8[:, 4:8, :], ADD))
+    wv(e_r4)
+    e_r2 = mark(V.tensor_tensor(T.R2[:, :, :], T.R4[:, 0:2, :], T.R4[:, 2:4, :], ADD))
+    wv(e_r2)
+    e_t = mark(V.tensor_tensor(T.TOT[:], T.R2[:, 0, :], T.R2[:, 1, :], ADD))
+
+    ws(e_t)
+    e_sd = mark(S.activation(T.sd[:], T.TOT[:, 0:n], ACT.Sqrt, bias=0.01, scale=1.0 / 1024))
+    wv(e_t, e_s3)
+    e_cv = mark(V.tensor_scalar(T.cv[:], T.TOT[:, n:2 * n], -1.0 / 1024, None, MUL))
+    e_o1 = mark(V.tensor_scalar(T.OD[:], S3[:, n:3 * n], -1.0 / 8, None, MUL))
+    wv(e_o1)
+    e_od = mark(V.tensor_tensor(T.OD[:], T.OD[:], G[:, r, n:3 * n], ADD))
+    wv(e_od)
+    e_dg = [mark(V.tensor_scalar(pd[j][:, 0:128], pd[j][:, 0:128], T.OD[:, n + j:n + j + 1], None, ADD))
+            for j in range(n)]
+    wv(e_sd)
+    e_rs = mark(V.reciprocal(T.rs[:], T.sd[:]))
+    wv(e_rs)
+    e_r2s = mark(V.tensor_tensor(T.rs2[:], T.rs[:], T.rs[:], MUL))
+    wv(e_r2s, e_cv)
+    e_be = mark(V.tensor_tensor(T.be[:], T.rs2[:], T.cv[:], MUL))
+
+    ws(e_rs, ci)
+    e_di = [mark(S.activation(ch(T.dg, j), T.idn[:], ACT.Copy, scale=T.rs[:, j:j + 1])) for j in range(n)]
+    wv(e_be)
+    e_st = []
+    for j in range(n):
+        e_u = mark(V.tensor_scalar(ch(T.ub, j), ch(T.xc, j), T.OD[:, j:j + 1], T.be[:, j:j + 1], ADD, MUL))
+        wv(e_u, e_dg[j])
+        e_v = mark(V.tensor_tensor(ch(T.vb, j), pd[j][:, 0:128], ch(T.ub, j), ADD))
+        wp(e_v, e_di[j])
+        e_m = mark(PE.matmul(px[j][:, 0:128], ch(T.vb, j), ch(T.dg, j), True, True))
+        ws(e_m)
+        e_c = mark(S.activation(ch(T.ob, j), px[j][:, 0:128], ACT.Copy))
+        wy(e_c)
+        e_st.append(mark(SY.dma_start(ch(T.dx, j), ch(T.ob, j)), 16))
+
+    g.wait_ge(T.sem.sent, ne)
+    wg(*[e for e in evs if not e[3]])
+    wg(*e_st)

@@ -3,7 +3,7 @@ from concourse.mybir import AluOpType, AxisListType, ActivationFunctionType
 
 NR = 8
 NCH = 4
-W = 5 * NCH
+W = 4 * NCH
 NEV = 120
 
 SCRATCH = {
@@ -21,14 +21,14 @@ SCRATCH = {
     "G": ("sbuf", [128, NR, W], "float32"),
     "S1": ("sbuf", [128, 4, W], "float32"),
     "S2": ("sbuf", [128, 2, W], "float32"),
-    "S3": ("sbuf", [128, 3 * NCH], "float32"),
-    "DD": ("sbuf", [128, 7, 3 * NCH], "float32"),
-    "DW": ("sbuf", [128, 7, 2 * NCH], "float32"),
+    "S3": ("sbuf", [128, W], "float32"),
+    "DD": ("sbuf", [128, 7, W], "float32"),
+    "DW": ("sbuf", [128, 7, NCH], "float32"),
     "Q8": ("sbuf", [128, 8, 2 * NCH], "float32"),
     "R4": ("sbuf", [128, 4, 2 * NCH], "float32"),
     "R2": ("sbuf", [128, 2, 2 * NCH], "float32"),
     "TOT": ("sbuf", [128, 2 * NCH], "float32"),
-    "OD": ("sbuf", [128, 2 * NCH], "float32"),
+    "OD": ("sbuf", [128, W], "float32"),
     "sd": ("sbuf", [128, NCH], "float32"),
     "rs": ("sbuf", [128, NCH], "float32"),
     "rs2": ("sbuf", [128, NCH], "float32"),
@@ -53,6 +53,20 @@ def _low_bits(mask, n):
             n -= 1
         b <<= 1
     return out
+
+
+def _send(g, T, topo, core, dsts, ap, nmax):
+    m = topo.mask(core, dsts[0])
+    for d in dsts:
+        m &= topo.mask(core, d)
+    m = _low_bits(m, nmax)
+    ids = []
+    for d in dsts:
+        rid, pid = topo.addr(d, core)
+        ids.append(DstId(rid=rid, pnc=pid))
+    g.remote_dma_fused([RemoteDMATransfer(dst_ids=ids, dma_engine_mask=m, remote_sem=T.sem.arr,
+                                          srcs=[ap], dsts=[ap for _ in dsts], alu_op=0)], local_sem=T.sem.sent)
+    return bin(m).count("1")
 
 
 def rank_program(g, core, T, topo):
@@ -102,10 +116,10 @@ def rank_program(g, core, T, topo):
 
     px = [T["px%d" % j] for j in range(n)]
     pd = [T["pd%d" % j] for j in range(n)]
-    own = []
+    own_x, own_d = [], []
 
     wp(cp, c1, lx0, lx1)
-    ex = [mark(PE.matmul(px[j][:, 0:130], ch(T.xs, j), T.pm[:, 0:130], True, True)) for j in range(n)]
+    ex = [mark(PE.matmul(px[j][:, 0:129], ch(T.xs, j), T.pm[:, 0:129], True, True)) for j in range(n)]
     wp(ld0, ld1)
     ed = [mark(PE.matmul(pd[j][:, 0:129], ch(T.ds, j), T.pm[:, 0:129], True, True)) for j in range(n)]
 
@@ -113,53 +127,48 @@ def rank_program(g, core, T, topo):
     for j in range(n):
         ws(ex[j])
         exc.append(mark(S.activation(ch(T.xc, j), px[j][:, 0:128], ACT.Copy)))
-        own.append(mark(S.activation(ch(T.junk, j), px[j][:, 0:128], ACT.Square,
-                                     accum_out=T.G[:, r, 3 * n + j:3 * n + j + 1])))
-        own.append(mark(S.activation(T.G[:, r, j:j + n + 1:n], px[j][:, 128:130], ACT.Copy)))
+        own_x.append(mark(S.activation(ch(T.junk, j), px[j][:, 0:128], ACT.Square,
+                                       accum_out=T.G[:, r, n + j:n + j + 1])))
+        own_x.append(mark(S.activation(T.G[:, r, j:j + 1], px[j][:, 128:129], ACT.Copy)))
 
     for j in range(n):
         wv(ed[j], exc[j])
         ep = mark(V.tensor_tensor(ch(T.prod, j), pd[j][:, 0:128], ch(T.xc, j), MUL))
-        own.append(mark(V.tensor_copy(T.G[:, r, 2 * n + j:2 * n + j + 1], pd[j][:, 128:129])))
+        own_d.append(mark(V.tensor_copy(T.G[:, r, 3 * n + j:3 * n + j + 1], pd[j][:, 128:129])))
         wv(ep)
-        own.append(mark(V.tensor_reduce(T.G[:, r, 4 * n + j:4 * n + j + 1], ch(T.prod, j), AxisListType.X, ADD)))
+        own_d.append(mark(V.tensor_reduce(T.G[:, r, 2 * n + j:2 * n + j + 1], ch(T.prod, j), AxisListType.X, ADD)))
 
-    dsts = [T.cores[(r + k) % NR] for k in range(1, NR)]
-    m = topo.mask(core, dsts[0])
-    for d in dsts:
-        m &= topo.mask(core, d)
-    m = _low_bits(m, 8)
-    ne = bin(m).count("1")
-    ids = []
-    for d in dsts:
-        rid, pid = topo.addr(d, core)
-        ids.append(DstId(rid=rid, pnc=pid))
-    wg(*own)
-    g.remote_dma_fused([RemoteDMATransfer(dst_ids=ids, dma_engine_mask=m, remote_sem=T.sem.arr,
-                                          srcs=[T.G[:, r, :]], dsts=[T.G[:, r, :] for _ in dsts], alu_op=0)],
-                       local_sem=T.sem.sent)
+    nxt = [T.cores[(r + 1) % NR]]
+    rest = [T.cores[(r + k) % NR] for k in range(2, NR)]
+    wg(*own_x)
+    ne = _send(g, T, topo, core, nxt, T.G[:, r, 0:2 * n], 8)
+    wg(*own_d)
+    _send(g, T, topo, core, rest, T.G[:, r, :], 8)
+    _send(g, T, topo, core, nxt, T.G[:, r, 2 * n:4 * n], 8)
 
-    wv(*own)
-    V.wait_ge(T.sem.arr, 7 * ne)
+    wv(*own_x)
+    wv(*own_d)
+    V.wait_ge(T.sem.arr, 8 * ne)
     G, S1, S2, S3, DD, DW, Q8 = T.G, T.S1, T.S2, T.S3, T.DD, T.DW, T.Q8
     e_s1 = mark(V.tensor_tensor(S1[:, :, :], G[:, 0:4, :], G[:, 4:8, :], ADD))
-    e_d1 = mark(V.tensor_tensor(DD[:, 0:4, :], G[:, 0:4, 0:3 * n], G[:, 4:8, 0:3 * n], SUB))
+    e_d1 = mark(V.tensor_tensor(DD[:, 0:4, :], G[:, 0:4, :], G[:, 4:8, :], SUB))
     wv(e_s1)
     e_s2 = mark(V.tensor_tensor(S2[:, :, :], S1[:, 0:2, :], S1[:, 2:4, :], ADD))
-    e_d2 = mark(V.tensor_tensor(DD[:, 4:6, :], S1[:, 0:2, 0:3 * n], S1[:, 2:4, 0:3 * n], SUB))
+    e_d2 = mark(V.tensor_tensor(DD[:, 4:6, :], S1[:, 0:2, :], S1[:, 2:4, :], SUB))
     wv(e_s2)
-    e_d3 = mark(V.tensor_tensor(DD[:, 6, :], S2[:, 0, 0:3 * n], S2[:, 1, 0:3 * n], SUB))
-    e_s3 = mark(V.tensor_tensor(S3[:], S2[:, 0, 0:3 * n], S2[:, 1, 0:3 * n], ADD))
-    e_q7 = mark(V.tensor_tensor(Q8[:, 7, :], S2[:, 0, 3 * n:5 * n], S2[:, 1, 3 * n:5 * n], ADD))
+    e_d3 = mark(V.tensor_tensor(DD[:, 6, :], S2[:, 0, :], S2[:, 1, :], SUB))
+    e_s3 = mark(V.tensor_tensor(S3[:], S2[:, 0, :], S2[:, 1, :], ADD))
+    e_q7 = mark(V.tensor_tensor(Q8[:, 7, :], S2[:, 0, n:3 * n], S2[:, 1, n:3 * n], ADD))
     ws(e_d1)
-    e_w1 = mark(S.activation(DW[:, 0:4, :], DD[:, 0:4, 0:2 * n], ACT.Copy, scale=64.0))
+    e_w1 = mark(S.activation(DW[:, 0:4, :], DD[:, 0:4, 0:n], ACT.Copy, scale=64.0))
     ws(e_d2)
-    e_w2 = mark(S.activation(DW[:, 4:6, :], DD[:, 4:6, 0:2 * n], ACT.Copy, scale=32.0))
+    e_w2 = mark(S.activation(DW[:, 4:6, :], DD[:, 4:6, 0:n], ACT.Copy, scale=32.0))
     ws(e_d3)
-    e_w3 = mark(S.activation(DW[:, 6, :], DD[:, 6, 0:2 * n], ACT.Copy, scale=16.0))
+    e_w3 = mark(S.activation(DW[:, 6, :], DD[:, 6, 0:n], ACT.Copy, scale=16.0))
     wv(e_d1, e_d2, e_d3, e_w1, e_w2, e_w3)
-    e_q = mark(V.tensor_tensor(Q8[:, 0:7, :], DW[:, :, :], DD[:, :, n:3 * n], MUL))
-    wv(e_q, e_q7)
+    e_qa = mark(V.tensor_tensor(Q8[:, 0:7, 0:n], DW[:, :, :], DD[:, :, 0:n], MUL))
+    e_qb = mark(V.tensor_tensor(Q8[:, 0:7, n:2 * n], DW[:, :, :], DD[:, :, 3 * n:4 * n], MUL))
+    wv(e_qa, e_qb, e_q7)
     e_r4 = mark(V.tensor_tensor(T.R4[:, :, :], Q8[:, 0:4, :], Q8[:, 4:8, :], ADD))
     wv(e_r4)
     e_r2 = mark(V.tensor_tensor(T.R2[:, :, :], T.R4[:, 0:2, :], T.R4[:, 2:4, :], ADD))
@@ -170,11 +179,11 @@ def rank_program(g, core, T, topo):
     e_sd = mark(S.activation(T.sd[:], T.TOT[:, 0:n], ACT.Sqrt, bias=0.01, scale=1.0 / 1024))
     wv(e_t, e_s3)
     e_cv = mark(V.tensor_scalar(T.cv[:], T.TOT[:, n:2 * n], -1.0 / 1024, None, MUL))
-    e_o1 = mark(V.tensor_scalar(T.OD[:], S3[:, n:3 * n], -1.0 / 8, None, MUL))
+    e_o1 = mark(V.tensor_scalar(T.OD[:], S3[:], -1.0 / 8, None, MUL))
     wv(e_o1)
-    e_od = mark(V.tensor_tensor(T.OD[:], T.OD[:], G[:, r, n:3 * n], ADD))
+    e_od = mark(V.tensor_tensor(T.OD[:], T.OD[:], G[:, r, :], ADD))
     wv(e_od)
-    e_dg = [mark(V.tensor_scalar(pd[j][:, 0:128], pd[j][:, 0:128], T.OD[:, n + j:n + j + 1], None, ADD))
+    e_dg = [mark(V.tensor_scalar(pd[j][:, 0:128], pd[j][:, 0:128], T.OD[:, 3 * n + j:3 * n + j + 1], None, ADD))
             for j in range(n)]
     wv(e_sd)
     e_rs = mark(V.reciprocal(T.rs[:], T.sd[:]))
@@ -198,6 +207,6 @@ def rank_program(g, core, T, topo):
         wy(e_c)
         e_st.append(mark(SY.dma_start(ch(T.dx, j), ch(T.ob, j)), 16))
 
-    g.wait_ge(T.sem.sent, ne)
+    g.wait_ge(T.sem.sent, 3 * ne)
     wg(*[e for e in evs if not e[3]])
     wg(*e_st)

@@ -1,16 +1,18 @@
+import numpy as np
 from concourse.bass import DstId, RemoteDMATransfer
 from concourse.mybir import AluOpType, AxisListType, ActivationFunctionType
 
 NR = 8
 NCH = 4
-W = 4 * NCH
-NEV = 120
+H = 2 * NCH
+NEV = 118
+CS = float(np.float32(8.0 ** -0.5))
 
 SCRATCH = {
     "xs": ("sbuf", [128, 512], "float32"),
     "ds": ("sbuf", [128, 512], "float32"),
     "pm": ("sbuf", [128, 132], "float32"),
-    "idn": ("sbuf", [128, 128], "float32"),
+    "idn": ("sbuf", [128, 132], "float32"),
     "xc": ("sbuf", [128, 512], "float32"),
     "junk": ("sbuf", [128, 512], "float32"),
     "prod": ("sbuf", [128, 512], "float32"),
@@ -18,53 +20,39 @@ SCRATCH = {
     "vb": ("sbuf", [128, 512], "float32"),
     "dg": ("sbuf", [128, 512], "float32"),
     "ob": ("sbuf", [128, 512], "float32"),
-    "G": ("sbuf", [128, NR, W], "float32"),
-    "S1": ("sbuf", [128, 4, W], "float32"),
-    "S2": ("sbuf", [128, 2, W], "float32"),
-    "S3": ("sbuf", [128, W], "float32"),
-    "DD": ("sbuf", [128, 7, W], "float32"),
-    "DW": ("sbuf", [128, 7, NCH], "float32"),
-    "Q8": ("sbuf", [128, 8, 2 * NCH], "float32"),
-    "R4": ("sbuf", [128, 4, 2 * NCH], "float32"),
-    "R2": ("sbuf", [128, 2, 2 * NCH], "float32"),
-    "TOT": ("sbuf", [128, 2 * NCH], "float32"),
-    "OD": ("sbuf", [128, W], "float32"),
-    "sd": ("sbuf", [128, NCH], "float32"),
-    "rs": ("sbuf", [128, NCH], "float32"),
-    "rs2": ("sbuf", [128, NCH], "float32"),
-    "cv": ("sbuf", [128, NCH], "float32"),
-    "be": ("sbuf", [128, NCH], "float32"),
+    "GX": ("sbuf", [128, NR, H], "float32"),
+    "GD": ("sbuf", [128, NR, H], "float32"),
+    "X1": ("sbuf", [128, 4, H], "float32"),
+    "X2": ("sbuf", [128, 2, H], "float32"),
+    "X3": ("sbuf", [128, H], "float32"),
+    "D1": ("sbuf", [128, 4, H], "float32"),
+    "D2": ("sbuf", [128, 2, H], "float32"),
+    "D3": ("sbuf", [128, H], "float32"),
+    "DM": ("sbuf", [128, NR, NCH], "float32"),
+    "PR": ("sbuf", [128, NR, NCH], "float32"),
+    "J8": ("sbuf", [128, NCH, NR], "float32"),
 }
+for _nm in ("NS", "SM", "T2", "OX", "QV", "VE", "RS2", "NR2", "OXN", "RS", "BE", "TT", "KK"):
+    SCRATCH[_nm] = ("sbuf", [128, NCH], "float32")
 for _j in range(NCH):
     SCRATCH["px%d" % _j] = ("psum", [128, 512], "float32")
     SCRATCH["pd%d" % _j] = ("psum", [128, 512], "float32")
 
-SEMAPHORES = ["e%d" % _i for _i in range(NEV)] + ["arr", "sent"]
+SEMAPHORES = ["e%d" % _i for _i in range(NEV)] + ["arrx", "arrd", "sent"]
 
 ADD, SUB, MUL = AluOpType.add, AluOpType.subtract, AluOpType.mult
 ACT = ActivationFunctionType
 
 
-def _low_bits(mask, n):
-    out, b = 0, 1
-    while n > 0 and b <= mask:
-        if mask & b:
-            out |= b
-            n -= 1
-        b <<= 1
-    return out
-
-
-def _send(g, T, topo, core, dsts, ap, nmax):
+def _send(g, T, topo, core, dsts, ap, rsem):
     m = topo.mask(core, dsts[0])
     for d in dsts:
         m &= topo.mask(core, d)
-    m = _low_bits(m, nmax)
     ids = []
     for d in dsts:
         rid, pid = topo.addr(d, core)
         ids.append(DstId(rid=rid, pnc=pid))
-    g.remote_dma_fused([RemoteDMATransfer(dst_ids=ids, dma_engine_mask=m, remote_sem=T.sem.arr,
+    g.remote_dma_fused([RemoteDMATransfer(dst_ids=ids, dma_engine_mask=m, remote_sem=rsem,
                                           srcs=[ap], dsts=[ap for _ in dsts], alu_op=0)], local_sem=T.sem.sent)
     return bin(m).count("1")
 
@@ -101,6 +89,9 @@ def rank_program(g, core, T, topo):
     def ch(t, j):
         return t[:, 128 * j:128 * (j + 1)]
 
+    def col(t, j):
+        return t[:, j:j + 1]
+
     lx0 = mark(SY.dma_start(T.xs[0:64, :], T.x[0:64, :]), 16)
     lx1 = mark(S.dma_start(T.xs[64:128, :], T.x[64:128, :]), 16)
     ld0 = mark(SY.dma_start(T.ds[0:64, :], T.dy[0:64, :]), 16)
@@ -108,97 +99,100 @@ def rank_program(g, core, T, topo):
 
     c0 = mark(V.memset(T.pm[:, 0:128], -1.0 / 128))
     c1 = mark(V.memset(T.pm[:, 128:132], 1.0 / 128))
-    c2 = mark(V.memset(T.idn[:], 0.0))
+    c2 = mark(V.memset(T.idn[:, 0:128], 0.0))
+    c3 = mark(V.memset(T.idn[:, 128:132], -1.0 / 1024))
     wg(c0)
     cp = mark(g.affine_select(T.pm[:, 0:128], T.pm[:, 0:128], [[-1, 128]], AluOpType.not_equal, 127.0 / 128, 0, 1))
     wg(c2)
-    ci = mark(g.affine_select(T.idn[:], T.idn[:], [[-1, 128]], AluOpType.not_equal, 1.0, 0, 1))
+    ci = mark(g.affine_select(T.idn[:, 0:128], T.idn[:, 0:128], [[-1, 128]], AluOpType.not_equal, 1.0, 0, 1))
 
     px = [T["px%d" % j] for j in range(n)]
     pd = [T["pd%d" % j] for j in range(n)]
+    GX, GD = T.GX, T.GD
     own_x, own_d = [], []
 
     wp(cp, c1, lx0, lx1)
     ex = [mark(PE.matmul(px[j][:, 0:129], ch(T.xs, j), T.pm[:, 0:129], True, True)) for j in range(n)]
-    wp(ld0, ld1)
-    ed = [mark(PE.matmul(pd[j][:, 0:129], ch(T.ds, j), T.pm[:, 0:129], True, True)) for j in range(n)]
+    wp(ci, c3, ld0, ld1)
+    ed = [mark(PE.matmul(pd[j][:, 0:129], ch(T.ds, j), T.idn[:, 0:129], True, True)) for j in range(n)]
 
     exc = []
     for j in range(n):
         ws(ex[j])
+        own_x.append(mark(S.activation(ch(T.junk, j), px[j][:, 0:128], ACT.Square, accum_out=GX[:, r, n + j:n + j + 1])))
+        own_x.append(mark(S.activation(GX[:, r, j:j + 1], px[j][:, 128:129], ACT.Copy)))
         exc.append(mark(S.activation(ch(T.xc, j), px[j][:, 0:128], ACT.Copy)))
-        own_x.append(mark(S.activation(ch(T.junk, j), px[j][:, 0:128], ACT.Square,
-                                       accum_out=T.G[:, r, n + j:n + j + 1])))
-        own_x.append(mark(S.activation(T.G[:, r, j:j + 1], px[j][:, 128:129], ACT.Copy)))
 
     for j in range(n):
         wv(ed[j], exc[j])
         ep = mark(V.tensor_tensor(ch(T.prod, j), pd[j][:, 0:128], ch(T.xc, j), MUL))
-        own_d.append(mark(V.tensor_copy(T.G[:, r, 3 * n + j:3 * n + j + 1], pd[j][:, 128:129])))
+        ws(ep)
+        own_d.append(mark(S.activation(GD[:, r, n + j:n + j + 1], pd[j][:, 128:129], ACT.Copy)))
         wv(ep)
-        own_d.append(mark(V.tensor_reduce(T.G[:, r, 2 * n + j:2 * n + j + 1], ch(T.prod, j), AxisListType.X, ADD)))
+        own_d.append(mark(V.tensor_reduce(GD[:, r, j:j + 1], ch(T.prod, j), AxisListType.X, ADD)))
 
-    nxt = [T.cores[(r + 1) % NR]]
-    rest = [T.cores[(r + k) % NR] for k in range(2, NR)]
+    others = [T.cores[(r + k) % NR] for k in range(1, NR)]
     wg(*own_x)
-    ne = _send(g, T, topo, core, nxt, T.G[:, r, 0:2 * n], 8)
+    ne = _send(g, T, topo, core, others, GX[:, r, :], T.sem.arrx)
     wg(*own_d)
-    _send(g, T, topo, core, rest, T.G[:, r, :], 8)
-    _send(g, T, topo, core, nxt, T.G[:, r, 2 * n:4 * n], 8)
+    _send(g, T, topo, core, others, GD[:, r, :], T.sem.arrd)
 
     wv(*own_x)
-    wv(*own_d)
-    V.wait_ge(T.sem.arr, 8 * ne)
-    G, S1, S2, S3, DD, DW, Q8 = T.G, T.S1, T.S2, T.S3, T.DD, T.DW, T.Q8
-    e_s1 = mark(V.tensor_tensor(S1[:, :, :], G[:, 0:4, :], G[:, 4:8, :], ADD))
-    e_d1 = mark(V.tensor_tensor(DD[:, 0:4, :], G[:, 0:4, :], G[:, 4:8, :], SUB))
-    wv(e_s1)
-    e_s2 = mark(V.tensor_tensor(S2[:, :, :], S1[:, 0:2, :], S1[:, 2:4, :], ADD))
-    e_d2 = mark(V.tensor_tensor(DD[:, 4:6, :], S1[:, 0:2, :], S1[:, 2:4, :], SUB))
-    wv(e_s2)
-    e_d3 = mark(V.tensor_tensor(DD[:, 6, :], S2[:, 0, :], S2[:, 1, :], SUB))
-    e_s3 = mark(V.tensor_tensor(S3[:], S2[:, 0, :], S2[:, 1, :], ADD))
-    e_q7 = mark(V.tensor_tensor(Q8[:, 7, :], S2[:, 0, n:3 * n], S2[:, 1, n:3 * n], ADD))
-    ws(e_d1)
-    e_w1 = mark(S.activation(DW[:, 0:4, :], DD[:, 0:4, 0:n], ACT.Copy, scale=64.0))
-    ws(e_d2)
-    e_w2 = mark(S.activation(DW[:, 4:6, :], DD[:, 4:6, 0:n], ACT.Copy, scale=32.0))
-    ws(e_d3)
-    e_w3 = mark(S.activation(DW[:, 6, :], DD[:, 6, 0:n], ACT.Copy, scale=16.0))
-    wv(e_d1, e_d2, e_d3, e_w1, e_w2, e_w3)
-    e_qa = mark(V.tensor_tensor(Q8[:, 0:7, 0:n], DW[:, :, :], DD[:, :, 0:n], MUL))
-    e_qb = mark(V.tensor_tensor(Q8[:, 0:7, n:2 * n], DW[:, :, :], DD[:, :, 3 * n:4 * n], MUL))
-    wv(e_qa, e_qb, e_q7)
-    e_r4 = mark(V.tensor_tensor(T.R4[:, :, :], Q8[:, 0:4, :], Q8[:, 4:8, :], ADD))
-    wv(e_r4)
-    e_r2 = mark(V.tensor_tensor(T.R2[:, :, :], T.R4[:, 0:2, :], T.R4[:, 2:4, :], ADD))
+    V.wait_ge(T.sem.arrx, 7 * ne)
+    a1 = mark(V.tensor_tensor(T.X1[:, :, :], GX[:, 0:4, :], GX[:, 4:8, :], ADD))
+    wv(a1)
+    a2 = mark(V.tensor_tensor(T.X2[:, :, :], T.X1[:, 0:2, :], T.X1[:, 2:4, :], ADD))
+    wv(a2)
+    a3 = mark(V.tensor_tensor(T.X3[:], T.X2[:, 0, :], T.X2[:, 1, :], ADD))
+    wv(a3)
+    e_ns = mark(V.tensor_scalar(T.NS[:], T.X3[:, 0:n], -CS / 8, None, MUL))
+    e_sm = mark(V.tensor_scalar(T.SM[:], T.X3[:, 0:n], 128.0, None, MUL))
+    e_t2 = mark(V.tensor_scalar(T.T2[:], T.X3[:, n:2 * n], 1.0 / 1024, 0.01, MUL, ADD))
+    ws(*own_x)
+    S.wait_ge(T.sem.arrx, 7 * ne)
+    ws(e_ns)
+    e_q = [mark(S.activation(T.J8[:, j, :], GX[:, :, j], ACT.Square, bias=col(T.NS, j), scale=CS,
+                             accum_out=col(T.QV, j))) for j in range(n)]
+    wv(e_sm)
+    e_dm = [mark(V.tensor_scalar(T.DM[:, :, j], GX[:, :, j], -1024.0, col(T.SM, j), MUL, ADD)) for j in range(n)]
+    wv(*e_dm)
+    e_ox = mark(V.tensor_scalar(T.OX[:], T.DM[:, r, :], -1.0 / 1024, None, MUL))
+    wv(e_t2, *e_q)
+    e_ve = mark(V.tensor_tensor(T.VE[:], T.QV[:], T.T2[:], ADD))
+    wv(e_ve)
+    e_r2 = mark(V.reciprocal(T.RS2[:], T.VE[:]))
+    ws(e_r2)
+    e_rs = mark(S.activation(T.RS[:], T.RS2[:], ACT.Sqrt))
     wv(e_r2)
-    e_t = mark(V.tensor_tensor(T.TOT[:], T.R2[:, 0, :], T.R2[:, 1, :], ADD))
-
-    ws(e_t)
-    e_sd = mark(S.activation(T.sd[:], T.TOT[:, 0:n], ACT.Sqrt, bias=0.01, scale=1.0 / 1024))
-    wv(e_t, e_s3)
-    e_cv = mark(V.tensor_scalar(T.cv[:], T.TOT[:, n:2 * n], -1.0 / 1024, None, MUL))
-    e_o1 = mark(V.tensor_scalar(T.OD[:], S3[:], -1.0 / 8, None, MUL))
-    wv(e_o1)
-    e_od = mark(V.tensor_tensor(T.OD[:], T.OD[:], G[:, r, :], ADD))
-    wv(e_od)
-    e_dg = [mark(V.tensor_scalar(pd[j][:, 0:128], pd[j][:, 0:128], T.OD[:, 3 * n + j:3 * n + j + 1], None, ADD))
-            for j in range(n)]
-    wv(e_sd)
-    e_rs = mark(V.reciprocal(T.rs[:], T.sd[:]))
-    wv(e_rs)
-    e_r2s = mark(V.tensor_tensor(T.rs2[:], T.rs[:], T.rs[:], MUL))
-    wv(e_r2s, e_cv)
-    e_be = mark(V.tensor_tensor(T.be[:], T.rs2[:], T.cv[:], MUL))
-
+    e_n2 = mark(V.tensor_scalar(T.NR2[:], T.RS2[:], -1.0 / 1024, None, MUL))
+    wv(e_n2, e_ox)
+    e_on = mark(V.tensor_tensor(T.OXN[:], T.OX[:], T.NR2[:], MUL))
     ws(e_rs, ci)
-    e_di = [mark(S.activation(ch(T.dg, j), T.idn[:], ACT.Copy, scale=T.rs[:, j:j + 1])) for j in range(n)]
-    wv(e_be)
+    e_di = [mark(S.activation(ch(T.dg, j), T.idn[:, 0:128], ACT.Copy, scale=col(T.RS, j))) for j in range(n)]
+
+    wv(*own_d)
+    V.wait_ge(T.sem.arrd, 7 * ne)
+    p1 = mark(V.tensor_tensor(T.PR[:, :, :], T.DM[:, :, :], GD[:, :, n:2 * n], MUL))
+    wv(p1)
+    V.wait_ge(T.sem.sent, 2 * ne)
+    p2 = mark(V.tensor_tensor(GD[:, :, 0:n], GD[:, :, 0:n], T.PR[:, :, :], ADD))
+    wv(p2)
+    p3 = mark(V.tensor_tensor(T.D1[:, :, :], GD[:, 0:4, :], GD[:, 4:8, :], ADD))
+    wv(p3)
+    p4 = mark(V.tensor_tensor(T.D2[:, :, :], T.D1[:, 0:2, :], T.D1[:, 2:4, :], ADD))
+    wv(p4)
+    p5 = mark(V.tensor_tensor(T.D3[:], T.D2[:, 0, :], T.D2[:, 1, :], ADD))
+    wv(p5, e_on)
+    e_be = mark(V.tensor_tensor(T.BE[:], T.D3[:, 0:n], T.NR2[:], MUL))
+    e_tt = mark(V.tensor_tensor(T.TT[:], T.D3[:, 0:n], T.OXN[:], MUL))
+    wv(e_tt)
+    e_kk = mark(V.tensor_tensor(T.KK[:], T.TT[:], T.D3[:, n:2 * n], ADD))
+    wv(e_be, e_kk)
+
     e_st = []
     for j in range(n):
-        e_u = mark(V.tensor_scalar(ch(T.ub, j), ch(T.xc, j), T.OD[:, j:j + 1], T.be[:, j:j + 1], ADD, MUL))
-        wv(e_u, e_dg[j])
+        e_u = mark(V.tensor_scalar(ch(T.ub, j), ch(T.xc, j), col(T.BE, j), col(T.KK, j), MUL, ADD))
+        wv(e_u)
         e_v = mark(V.tensor_tensor(ch(T.vb, j), pd[j][:, 0:128], ch(T.ub, j), ADD))
         wp(e_v, e_di[j])
         e_m = mark(PE.matmul(px[j][:, 0:128], ch(T.vb, j), ch(T.dg, j), True, True))
@@ -207,6 +201,8 @@ def rank_program(g, core, T, topo):
         wy(e_c)
         e_st.append(mark(SY.dma_start(ch(T.dx, j), ch(T.ob, j)), 16))
 
-    g.wait_ge(T.sem.sent, 3 * ne)
+    g.wait_ge(T.sem.sent, 2 * ne)
+    g.wait_ge(T.sem.arrx, 7 * ne)
+    g.wait_ge(T.sem.arrd, 7 * ne)
     wg(*[e for e in evs if not e[3]])
     wg(*e_st)

@@ -1,4 +1,3 @@
-import numpy as np
 from concourse.bass import DstId, RemoteDMATransfer
 from concourse.mybir import AluOpType, AxisListType, ActivationFunctionType
 
@@ -6,7 +5,6 @@ NR = 8
 NCH = 4
 H = 2 * NCH
 NEV = 118
-CS = float(np.float32(8.0 ** -0.5))
 
 SCRATCH = {
     "xs": ("sbuf", [128, 512], "float32"),
@@ -32,7 +30,9 @@ SCRATCH = {
     "PR": ("sbuf", [128, NR, NCH], "float32"),
     "J8": ("sbuf", [128, NCH, NR], "float32"),
 }
-for _nm in ("NS", "SM", "T2", "OX", "QV", "VE", "RS2", "NR2", "OXN", "RS", "BE", "TT", "KK"):
+for _nm in ("NS", "SM", "T2", "QV"):
+    SCRATCH[_nm] = ("sbuf", [128, H], "float32")
+for _nm in ("C8", "CS", "OX", "VE", "RS2", "NR2", "RS", "BE"):
     SCRATCH[_nm] = ("sbuf", [128, NCH], "float32")
 for _j in range(NCH):
     SCRATCH["px%d" % _j] = ("psum", [128, 512], "float32")
@@ -42,6 +42,10 @@ SEMAPHORES = ["e%d" % _i for _i in range(NEV)] + ["arrx", "arrd", "sent"]
 
 ADD, SUB, MUL = AluOpType.add, AluOpType.subtract, AluOpType.mult
 ACT = ActivationFunctionType
+
+
+def _mc(j):
+    return 4 * (j // 2) + (j % 2)
 
 
 def _send(g, T, topo, core, dsts, ap, rsem):
@@ -92,15 +96,20 @@ def rank_program(g, core, T, topo):
     def col(t, j):
         return t[:, j:j + 1]
 
-    lx0 = mark(SY.dma_start(T.xs[0:64, :], T.x[0:64, :]), 16)
-    lx1 = mark(S.dma_start(T.xs[64:128, :], T.x[64:128, :]), 16)
+    lx = []
+    for j in range(n):
+        lx.append((mark(SY.dma_start(T.xs[0:64, 128 * j:128 * (j + 1)], T.x[0:64, 128 * j:128 * (j + 1)]), 16),
+                   mark(S.dma_start(T.xs[64:128, 128 * j:128 * (j + 1)], T.x[64:128, 128 * j:128 * (j + 1)]), 16)))
     ld0 = mark(SY.dma_start(T.ds[0:64, :], T.dy[0:64, :]), 16)
     ld1 = mark(S.dma_start(T.ds[64:128, :], T.dy[64:128, :]), 16)
 
+    c4 = mark(V.memset(T.C8[:], 0.125))
     c0 = mark(V.memset(T.pm[:, 0:128], -1.0 / 128))
     c1 = mark(V.memset(T.pm[:, 128:132], 1.0 / 128))
     c2 = mark(V.memset(T.idn[:, 0:128], 0.0))
     c3 = mark(V.memset(T.idn[:, 128:132], -1.0 / 1024))
+    ws(c4)
+    e_cs = mark(S.activation(T.CS[:], T.C8[:], ACT.Sqrt))
     wg(c0)
     cp = mark(g.affine_select(T.pm[:, 0:128], T.pm[:, 0:128], [[-1, 128]], AluOpType.not_equal, 127.0 / 128, 0, 1))
     wg(c2)
@@ -111,16 +120,20 @@ def rank_program(g, core, T, topo):
     GX, GD = T.GX, T.GD
     own_x, own_d = [], []
 
-    wp(cp, c1, lx0, lx1)
-    ex = [mark(PE.matmul(px[j][:, 0:129], ch(T.xs, j), T.pm[:, 0:129], True, True)) for j in range(n)]
+    wp(cp, c1)
+    ex = []
+    for j in range(n):
+        wp(*lx[j])
+        ex.append(mark(PE.matmul(px[j][:, 0:129], ch(T.xs, j), T.pm[:, 0:129], True, True)))
     wp(ci, c3, ld0, ld1)
     ed = [mark(PE.matmul(pd[j][:, 0:129], ch(T.ds, j), T.idn[:, 0:129], True, True)) for j in range(n)]
 
     exc = []
     for j in range(n):
+        m = _mc(j)
         ws(ex[j])
-        own_x.append(mark(S.activation(ch(T.junk, j), px[j][:, 0:128], ACT.Square, accum_out=GX[:, r, n + j:n + j + 1])))
-        own_x.append(mark(S.activation(GX[:, r, j:j + 1], px[j][:, 128:129], ACT.Copy)))
+        own_x.append(mark(S.activation(ch(T.junk, j), px[j][:, 0:128], ACT.Square, accum_out=GX[:, r, m + 2:m + 3])))
+        own_x.append(mark(S.activation(GX[:, r, m:m + 1], px[j][:, 128:129], ACT.Copy)))
         exc.append(mark(S.activation(ch(T.xc, j), px[j][:, 0:128], ACT.Copy)))
 
     for j in range(n):
@@ -131,42 +144,47 @@ def rank_program(g, core, T, topo):
         wv(ep)
         own_d.append(mark(V.tensor_reduce(GD[:, r, j:j + 1], ch(T.prod, j), AxisListType.X, ADD)))
 
-    others = [T.cores[(r + k) % NR] for k in range(1, NR)]
+    nxt = [T.cores[(r + 1) % NR]]
+    rest = [T.cores[(r + k) % NR] for k in range(2, NR)]
+    wg(*own_x[0:4])
+    ne = _send(g, T, topo, core, nxt, GX[:, r, 0:4], T.sem.arrx)
     wg(*own_x)
-    ne = _send(g, T, topo, core, others, GX[:, r, :], T.sem.arrx)
+    _send(g, T, topo, core, rest, GX[:, r, :], T.sem.arrx)
+    _send(g, T, topo, core, nxt, GX[:, r, 4:8], T.sem.arrx)
     wg(*own_d)
-    _send(g, T, topo, core, others, GD[:, r, :], T.sem.arrd)
+    _send(g, T, topo, core, nxt + rest, GD[:, r, :], T.sem.arrd)
+    nax = 8 * ne
+    nsent = 4 * ne
 
     wv(*own_x)
-    V.wait_ge(T.sem.arrx, 7 * ne)
+    V.wait_ge(T.sem.arrx, nax)
     a1 = mark(V.tensor_tensor(T.X1[:, :, :], GX[:, 0:4, :], GX[:, 4:8, :], ADD))
     wv(a1)
     a2 = mark(V.tensor_tensor(T.X2[:, :, :], T.X1[:, 0:2, :], T.X1[:, 2:4, :], ADD))
     wv(a2)
     a3 = mark(V.tensor_tensor(T.X3[:], T.X2[:, 0, :], T.X2[:, 1, :], ADD))
-    wv(a3)
-    e_ns = mark(V.tensor_scalar(T.NS[:], T.X3[:, 0:n], -CS / 8, None, MUL))
-    e_sm = mark(V.tensor_scalar(T.SM[:], T.X3[:, 0:n], 128.0, None, MUL))
-    e_t2 = mark(V.tensor_scalar(T.T2[:], T.X3[:, n:2 * n], 1.0 / 1024, 0.01, MUL, ADD))
+    wv(a3, e_cs)
+    e_ns = mark(V.tensor_scalar(T.NS[:], T.X3[:], -0.125, col(T.CS, 0), MUL, MUL))
+    e_sm = mark(V.tensor_scalar(T.SM[:], T.X3[:], 128.0, None, MUL))
+    e_t2 = mark(V.tensor_scalar(T.T2[:], T.X3[:], 1.0 / 1024, 0.01, MUL, ADD))
     ws(*own_x)
-    S.wait_ge(T.sem.arrx, 7 * ne)
-    ws(e_ns)
-    e_q = [mark(S.activation(T.J8[:, j, :], GX[:, :, j], ACT.Square, bias=col(T.NS, j), scale=CS,
-                             accum_out=col(T.QV, j))) for j in range(n)]
+    S.wait_ge(T.sem.arrx, nax)
+    ws(e_ns, e_cs)
+    e_q = [mark(S.activation(T.J8[:, j, :], GX[:, :, _mc(j)], ACT.Square, bias=col(T.NS, _mc(j)), scale=col(T.CS, 0),
+                             accum_out=col(T.QV, _mc(j) + 2))) for j in range(n)]
     wv(e_sm)
-    e_dm = [mark(V.tensor_scalar(T.DM[:, :, j], GX[:, :, j], -1024.0, col(T.SM, j), MUL, ADD)) for j in range(n)]
+    e_dm = [mark(V.tensor_scalar(T.DM[:, :, j], GX[:, :, _mc(j)], -1024.0, col(T.SM, _mc(j)), MUL, ADD)) for j in range(n)]
     wv(*e_dm)
     e_ox = mark(V.tensor_scalar(T.OX[:], T.DM[:, r, :], -1.0 / 1024, None, MUL))
     wv(e_t2, *e_q)
-    e_ve = mark(V.tensor_tensor(T.VE[:], T.QV[:], T.T2[:], ADD))
-    wv(e_ve)
+    e_ve = [mark(V.tensor_tensor(T.VE[:, 2 * h:2 * h + 2], T.QV[:, 4 * h + 2:4 * h + 4], T.T2[:, 4 * h + 2:4 * h + 4], ADD))
+            for h in range(2)]
+    wv(*e_ve)
     e_r2 = mark(V.reciprocal(T.RS2[:], T.VE[:]))
     ws(e_r2)
     e_rs = mark(S.activation(T.RS[:], T.RS2[:], ACT.Sqrt))
     wv(e_r2)
     e_n2 = mark(V.tensor_scalar(T.NR2[:], T.RS2[:], -1.0 / 1024, None, MUL))
-    wv(e_n2, e_ox)
-    e_on = mark(V.tensor_tensor(T.OXN[:], T.OX[:], T.NR2[:], MUL))
     ws(e_rs, ci)
     e_di = [mark(S.activation(ch(T.dg, j), T.idn[:, 0:128], ACT.Copy, scale=col(T.RS, j))) for j in range(n)]
 
@@ -174,7 +192,7 @@ def rank_program(g, core, T, topo):
     V.wait_ge(T.sem.arrd, 7 * ne)
     p1 = mark(V.tensor_tensor(T.PR[:, :, :], T.DM[:, :, :], GD[:, :, n:2 * n], MUL))
     wv(p1)
-    V.wait_ge(T.sem.sent, 2 * ne)
+    V.wait_ge(T.sem.sent, nsent)
     p2 = mark(V.tensor_tensor(GD[:, :, 0:n], GD[:, :, 0:n], T.PR[:, :, :], ADD))
     wv(p2)
     p3 = mark(V.tensor_tensor(T.D1[:, :, :], GD[:, 0:4, :], GD[:, 4:8, :], ADD))
@@ -182,27 +200,33 @@ def rank_program(g, core, T, topo):
     p4 = mark(V.tensor_tensor(T.D2[:, :, :], T.D1[:, 0:2, :], T.D1[:, 2:4, :], ADD))
     wv(p4)
     p5 = mark(V.tensor_tensor(T.D3[:], T.D2[:, 0, :], T.D2[:, 1, :], ADD))
-    wv(p5, e_on)
+    wv(p5, e_n2)
     e_be = mark(V.tensor_tensor(T.BE[:], T.D3[:, 0:n], T.NR2[:], MUL))
-    e_tt = mark(V.tensor_tensor(T.TT[:], T.D3[:, 0:n], T.OXN[:], MUL))
-    wv(e_tt)
-    e_kk = mark(V.tensor_tensor(T.KK[:], T.TT[:], T.D3[:, n:2 * n], ADD))
-    wv(e_be, e_kk)
+    ws(p5)
+    e_dq = [mark(S.activation(pd[j][:, 0:128], pd[j][:, 0:128], ACT.Identity, bias=col(T.D3, n + j))) for j in range(n)]
+    wv(e_be, e_ox)
 
     e_st = []
     for j in range(n):
-        e_u = mark(V.tensor_scalar(ch(T.ub, j), ch(T.xc, j), col(T.BE, j), col(T.KK, j), MUL, ADD))
-        wv(e_u)
+        e_u = mark(V.tensor_scalar(ch(T.ub, j), ch(T.xc, j), col(T.OX, j), col(T.BE, j), ADD, MUL))
+        wv(e_u, e_dq[j])
         e_v = mark(V.tensor_tensor(ch(T.vb, j), pd[j][:, 0:128], ch(T.ub, j), ADD))
         wp(e_v, e_di[j])
-        e_m = mark(PE.matmul(px[j][:, 0:128], ch(T.vb, j), ch(T.dg, j), True, True))
-        ws(e_m)
-        e_c = mark(S.activation(ch(T.ob, j), px[j][:, 0:128], ACT.Copy))
-        wy(e_c)
-        e_st.append(mark(SY.dma_start(ch(T.dx, j), ch(T.ob, j)), 16))
+        if j < n - 1:
+            parts = [(px[j], 0, 128)]
+        else:
+            parts = [(px[j], 0, 64), (pd[0], 64, 64)]
+        for bank, p0, w in parts:
+            c0_ = 128 * j + p0
+            e_m = mark(PE.matmul(bank[:, 0:w], T.vb[p0:p0 + w, 128 * j:128 * (j + 1)], T.dg[p0:p0 + w, c0_:c0_ + w],
+                                 True, True))
+            ws(e_m)
+            e_c = mark(S.activation(T.ob[:, c0_:c0_ + w], bank[:, 0:w], ACT.Copy))
+            wy(e_c)
+            e_st.append(mark(SY.dma_start(T.dx[:, c0_:c0_ + w], T.ob[:, c0_:c0_ + w]), 16))
 
-    g.wait_ge(T.sem.sent, 2 * ne)
-    g.wait_ge(T.sem.arrx, 7 * ne)
+    g.wait_ge(T.sem.sent, nsent)
+    g.wait_ge(T.sem.arrx, nax)
     g.wait_ge(T.sem.arrd, 7 * ne)
     wg(*[e for e in evs if not e[3]])
     wg(*e_st)

@@ -19,15 +19,14 @@ SCRATCH = {
     "dg": ("sbuf", [128, 512], "float32"),
     "ob": ("sbuf", [128, 512], "float32"),
     "GX": ("sbuf", [128, NR, H], "float32"),
-    "GD": ("sbuf", [128, NR, H], "float32"),
+    "GD": ("sbuf", [128, 2 * NR, H], "float32"),
     "X1": ("sbuf", [128, 4, H], "float32"),
     "X2": ("sbuf", [128, 2, H], "float32"),
     "X3": ("sbuf", [128, H], "float32"),
-    "D1": ("sbuf", [128, 4, H], "float32"),
-    "D2": ("sbuf", [128, 2, H], "float32"),
     "D3": ("sbuf", [128, H], "float32"),
     "DM": ("sbuf", [128, NR, NCH], "float32"),
-    "PR": ("sbuf", [128, NR, NCH], "float32"),
+    "JA": ("sbuf", [128, NCH, NR], "float32"),
+    "JB": ("sbuf", [128, NCH, 2 * NR], "float32"),
     "J8": ("sbuf", [128, NCH, NR], "float32"),
 }
 for _nm in ("NS", "SM", "T2", "QV"):
@@ -45,7 +44,7 @@ ACT = ActivationFunctionType
 
 
 def _mc(j):
-    return 4 * (j // 2) + (j % 2)
+    return 2 * j
 
 
 def _send(g, T, topo, core, dsts, ap, rsem):
@@ -132,7 +131,7 @@ def rank_program(g, core, T, topo):
     for j in range(n):
         m = _mc(j)
         ws(ex[j])
-        own_x.append(mark(S.activation(ch(T.junk, j), px[j][:, 0:128], ACT.Square, accum_out=GX[:, r, m + 2:m + 3])))
+        own_x.append(mark(S.activation(ch(T.junk, j), px[j][:, 0:128], ACT.Square, accum_out=GX[:, r, m + 1:m + 2])))
         own_x.append(mark(S.activation(GX[:, r, m:m + 1], px[j][:, 128:129], ACT.Copy)))
         exc.append(mark(S.activation(ch(T.xc, j), px[j][:, 0:128], ACT.Copy)))
 
@@ -140,19 +139,19 @@ def rank_program(g, core, T, topo):
         wv(ed[j], exc[j])
         ep = mark(V.tensor_tensor(ch(T.prod, j), pd[j][:, 0:128], ch(T.xc, j), MUL))
         ws(ep)
-        own_d.append(mark(S.activation(GD[:, r, n + j:n + j + 1], pd[j][:, 128:129], ACT.Copy)))
+        own_d.append(mark(S.activation(GD[:, 2 * r, n + j:n + j + 1], pd[j][:, 128:129], ACT.Copy)))
         wv(ep)
-        own_d.append(mark(V.tensor_reduce(GD[:, r, j:j + 1], ch(T.prod, j), AxisListType.X, ADD)))
+        own_d.append(mark(V.tensor_reduce(GD[:, 2 * r, j:j + 1], ch(T.prod, j), AxisListType.X, ADD)))
 
     nxt = [T.cores[(r + 1) % NR]]
     rest = [T.cores[(r + k) % NR] for k in range(2, NR)]
-    wg(*own_x[0:4])
-    ne = _send(g, T, topo, core, nxt, GX[:, r, 0:4], T.sem.arrx)
+    wg(*own_x[0:2])
+    ne = _send(g, T, topo, core, nxt, GX[:, r, 0:2], T.sem.arrx)
     wg(*own_x)
     _send(g, T, topo, core, rest, GX[:, r, :], T.sem.arrx)
-    _send(g, T, topo, core, nxt, GX[:, r, 4:8], T.sem.arrx)
+    _send(g, T, topo, core, nxt, GX[:, r, 2:8], T.sem.arrx)
     wg(*own_d)
-    _send(g, T, topo, core, nxt + rest, GD[:, r, :], T.sem.arrd)
+    _send(g, T, topo, core, nxt + rest, GD[:, 2 * r, :], T.sem.arrd)
     nax = 8 * ne
     nsent = 4 * ne
 
@@ -171,15 +170,14 @@ def rank_program(g, core, T, topo):
     S.wait_ge(T.sem.arrx, nax)
     ws(e_ns, e_cs)
     e_q = [mark(S.activation(T.J8[:, j, :], GX[:, :, _mc(j)], ACT.Square, bias=col(T.NS, _mc(j)), scale=col(T.CS, 0),
-                             accum_out=col(T.QV, _mc(j) + 2))) for j in range(n)]
+                             accum_out=col(T.QV, _mc(j) + 1))) for j in range(n)]
     wv(e_sm)
     e_dm = [mark(V.tensor_scalar(T.DM[:, :, j], GX[:, :, _mc(j)], -1024.0, col(T.SM, _mc(j)), MUL, ADD)) for j in range(n)]
     wv(*e_dm)
     e_ox = mark(V.tensor_scalar(T.OX[:], T.DM[:, r, :], -1.0 / 1024, None, MUL))
     wv(e_t2, *e_q)
-    e_ve = [mark(V.tensor_tensor(T.VE[:, 2 * h:2 * h + 2], T.QV[:, 4 * h + 2:4 * h + 4], T.T2[:, 4 * h + 2:4 * h + 4], ADD))
-            for h in range(2)]
-    wv(*e_ve)
+    e_ve = mark(V.tensor_tensor(T.VE[:], T.QV[:, 1:H:2], T.T2[:, 1:H:2], ADD))
+    wv(e_ve)
     e_r2 = mark(V.reciprocal(T.RS2[:], T.VE[:]))
     ws(e_r2)
     e_rs = mark(S.activation(T.RS[:], T.RS2[:], ACT.Sqrt))
@@ -190,24 +188,23 @@ def rank_program(g, core, T, topo):
 
     wv(*own_d)
     V.wait_ge(T.sem.arrd, 7 * ne)
-    p1 = mark(V.tensor_tensor(T.PR[:, :, :], T.DM[:, :, :], GD[:, :, n:2 * n], MUL))
-    wv(p1)
-    V.wait_ge(T.sem.sent, nsent)
-    p2 = mark(V.tensor_tensor(GD[:, :, 0:n], GD[:, :, 0:n], T.PR[:, :, :], ADD))
-    wv(p2)
-    p3 = mark(V.tensor_tensor(T.D1[:, :, :], GD[:, 0:4, :], GD[:, 4:8, :], ADD))
-    wv(p3)
-    p4 = mark(V.tensor_tensor(T.D2[:, :, :], T.D1[:, 0:2, :], T.D1[:, 2:4, :], ADD))
-    wv(p4)
-    p5 = mark(V.tensor_tensor(T.D3[:], T.D2[:, 0, :], T.D2[:, 1, :], ADD))
-    wv(p5, e_n2)
-    e_be = mark(V.tensor_tensor(T.BE[:], T.D3[:, 0:n], T.NR2[:], MUL))
-    ws(p5)
-    e_dq = [mark(S.activation(pd[j][:, 0:128], pd[j][:, 0:128], ACT.Identity, bias=col(T.D3, n + j))) for j in range(n)]
-    wv(e_be, e_ox)
+    p1 = mark(V.tensor_tensor(GD[:, 1:2 * NR:2, 0:n], T.DM[:, :, :], GD[:, 0:2 * NR:2, n:2 * n], MUL))
+    ws(*own_d)
+    S.wait_ge(T.sem.arrd, 7 * ne)
+    ws(e_n2)
+    e_be, e_dq = [], []
+    for j in range(n):
+        e_a = mark(S.activation(T.JA[:, j, :], GD[:, 0:2 * NR:2, n + j], ACT.Copy, accum_out=col(T.D3, n + j)))
+        ws(p1)
+        e_be.append(mark(S.activation(T.JB[:, j, :], GD[:, :, j], ACT.Copy, scale=col(T.NR2, j),
+                                      accum_out=col(T.BE, j))))
+        ws(e_a)
+        e_dq.append(mark(S.activation(pd[j][:, 0:128], pd[j][:, 0:128], ACT.Identity, bias=col(T.D3, n + j))))
+    wv(e_ox)
 
     e_st = []
     for j in range(n):
+        wv(e_be[j])
         e_u = mark(V.tensor_scalar(ch(T.ub, j), ch(T.xc, j), col(T.OX, j), col(T.BE, j), ADD, MUL))
         wv(e_u, e_dq[j])
         e_v = mark(V.tensor_tensor(ch(T.vb, j), pd[j][:, 0:128], ch(T.ub, j), ADD))

from concourse.bass import DstId, RemoteDMATransfer
from concourse.mybir import AluOpType, AxisListType, ActivationFunctionType

NR = 8
NCH = 4
H = 2 * NCH
NEV = 118

SCRATCH = {
    "xs": ("sbuf", [128, 512], "float32"),
    "ds": ("sbuf", [128, 512], "float32"),
    "pm": ("sbuf", [128, 132], "float32"),
    "idn": ("sbuf", [128, 132], "float32"),
    "xc": ("sbuf", [128, 512], "float32"),
    "junk": ("sbuf", [128, 512], "float32"),
    "prod": ("sbuf", [128, 512], "float32"),
    "ub": ("sbuf", [128, 512], "float32"),
    "vb": ("sbuf", [128, 512], "float32"),
    "dg": ("sbuf", [128, 512], "float32"),
    "ob": ("sbuf", [128, 512], "float32"),
    "GX": ("sbuf", [128, NR, H], "float32"),
    "GD": ("sbuf", [128, 2 * NR, H], "float32"),
    "X1": ("sbuf", [128, 4, H], "float32"),
    "X2": ("sbuf", [128, 2, H], "float32"),
    "X3": ("sbuf", [128, H], "float32"),
    "D3": ("sbuf", [128, H], "float32"),
    "DM": ("sbuf", [128, NR, NCH], "float32"),
    "JA": ("sbuf", [128, NCH, NR], "float32"),
    "JB": ("sbuf", [128, NCH, 2 * NR], "float32"),
    "J8": ("sbuf", [128, NCH, NR], "float32"),
}
for _nm in ("NS", "SM", "T2", "QV"):
    SCRATCH[_nm] = ("sbuf", [128, H], "float32")
for _nm in ("C8", "CS", "OX", "VE", "RS2", "NR2", "RS", "BE"):
    SCRATCH[_nm] = ("sbuf", [128, NCH], "float32")
for _j in range(NCH):
    SCRATCH["px%d" % _j] = ("psum", [128, 512], "float32")
    SCRATCH["pd%d" % _j] = ("psum", [128, 512], "float32")

SEMAPHORES = ["e%d" % _i for _i in range(NEV)] + ["arrx", "arrd", "sent"]

ADD, SUB, MUL = AluOpType.add, AluOpType.subtract, AluOpType.mult
ACT = ActivationFunctionType


def _mc(j):
    return 2 * j


def _send(g, T, topo, core, dsts, ap, rsem):
    m = topo.mask(core, dsts[0])
    for d in dsts:
        m &= topo.mask(core, d)
    ids = []
    for d in dsts:
        rid, pid = topo.addr(d, core)
        ids.append(DstId(rid=rid, pnc=pid))
    g.remote_dma_fused([RemoteDMATransfer(dst_ids=ids, dma_engine_mask=m, remote_sem=rsem,
                                          srcs=[ap], dsts=[ap for _ in dsts], alu_op=0)], local_sem=T.sem.sent)
    return bin(m).count("1")


def rank_program(g, core, T, topo):
    r = T.rank_of(core)
    if r is None:
        return
    n = NCH
    V, S, PE, SY = g.vector, g.scalar, g.tensor, g.sync
    evs = []
    seen = {}

    def mark(ins, k=1):
        e = [T.sem["e%d" % len(evs)], k, len(evs), False]
        evs.append(e)
        ins.then_inc(e[0], k)
        return e

    def wait(q, qn, *es):
        for e in es:
            if (qn, e[2]) in seen:
                continue
            seen[(qn, e[2])] = True
            e[3] = True
            q.wait_ge(e[0], e[1])

    def wv(*es): wait(V, "v", *es)
    def ws(*es): wait(S, "s", *es)
    def wp(*es): wait(PE, "p", *es)
    def wg(*es): wait(g, "g", *es)
    def wy(*es): wait(SY, "y", *es)

    def ch(t, j):
        return t[:, 128 * j:128 * (j + 1)]

    def col(t, j):
        return t[:, j:j + 1]

    lx = []
    for j in range(n):
        lx.append((mark(SY.dma_start(T.xs[0:64, 128 * j:128 * (j + 1)], T.x[0:64, 128 * j:128 * (j + 1)]), 16),
                   mark(S.dma_start(T.xs[64:128, 128 * j:128 * (j + 1)], T.x[64:128, 128 * j:128 * (j + 1)]), 16)))
    ld0 = mark(SY.dma_start(T.ds[0:64, :], T.dy[0:64, :]), 16)
    ld1 = mark(S.dma_start(T.ds[64:128, :], T.dy[64:128, :]), 16)

    c4 = mark(V.memset(T.C8[:], 0.125))
    c0 = mark(V.memset(T.pm[:, 0:128], -1.0 / 128))
    c1 = mark(V.memset(T.pm[:, 128:132], 1.0 / 128))
    c2 = mark(V.memset(T.idn[:, 0:128], 0.0))
    c3 = mark(V.memset(T.idn[:, 128:132], -1.0 / 1024))
    ws(c4)
    e_cs = mark(S.activation(T.CS[:], T.C8[:], ACT.Sqrt))
    wg(c0)
    cp = mark(g.affine_select(T.pm[:, 0:128], T.pm[:, 0:128], [[-1, 128]], AluOpType.not_equal, 127.0 / 128, 0, 1))
    wg(c2)
    ci = mark(g.affine_select(T.idn[:, 0:128], T.idn[:, 0:128], [[-1, 128]], AluOpType.not_equal, 1.0, 0, 1))

    px = [T["px%d" % j] for j in range(n)]
    pd = [T["pd%d" % j] for j in range(n)]
    GX, GD = T.GX, T.GD
    own_x, own_d = [], []

    wp(cp, c1)
    ex = []
    for j in range(n):
        wp(*lx[j])
        ex.append(mark(PE.matmul(px[j][:, 0:129], ch(T.xs, j), T.pm[:, 0:129], True, True)))
    wp(ci, c3, ld0, ld1)
    ed = [mark(PE.matmul(pd[j][:, 0:129], ch(T.ds, j), T.idn[:, 0:129], True, True)) for j in range(n)]

    exc = []
    for j in range(n):
        m = _mc(j)
        ws(ex[j])
        own_x.append(mark(S.activation(ch(T.junk, j), px[j][:, 0:128], ACT.Square, accum_out=GX[:, r, m + 1:m + 2])))
        own_x.append(mark(S.activation(GX[:, r, m:m + 1], px[j][:, 128:129], ACT.Copy)))
        exc.append(mark(S.activation(ch(T.xc, j), px[j][:, 0:128], ACT.Copy)))

    for j in range(n):
        wv(ed[j], exc[j])
        ep = mark(V.tensor_tensor(ch(T.prod, j), pd[j][:, 0:128], ch(T.xc, j), MUL))
        ws(ep)
        own_d.append(mark(S.activation(GD[:, 2 * r, n + j:n + j + 1], pd[j][:, 128:129], ACT.Copy)))
        wv(ep)
        own_d.append(mark(V.tensor_reduce(GD[:, 2 * r, j:j + 1], ch(T.prod, j), AxisListType.X, ADD)))

    nxt = [T.cores[(r + 1) % NR]]
    rest = [T.cores[(r + k) % NR] for k in range(2, NR)]
    wg(*own_x[0:2])
    ne = _send(g, T, topo, core, nxt, GX[:, r, 0:2], T.sem.arrx)
    wg(*own_x)
    _send(g, T, topo, core, rest, GX[:, r, :], T.sem.arrx)
    _send(g, T, topo, core, nxt, GX[:, r, 2:8], T.sem.arrx)
    wg(*own_d)
    _send(g, T, topo, core, nxt + rest, GD[:, 2 * r, :], T.sem.arrd)
    nax = 8 * ne
    nsent = 4 * ne

    wv(*own_x)
    V.wait_ge(T.sem.arrx, nax)
    a1 = mark(V.tensor_tensor(T.X1[:, :, :], GX[:, 0:4, :], GX[:, 4:8, :], ADD))
    wv(a1)
    a2 = mark(V.tensor_tensor(T.X2[:, :, :], T.X1[:, 0:2, :], T.X1[:, 2:4, :], ADD))
    wv(a2)
    a3 = mark(V.tensor_tensor(T.X3[:], T.X2[:, 0, :], T.X2[:, 1, :], ADD))
    wv(a3, e_cs)
    e_ns = mark(V.tensor_scalar(T.NS[:], T.X3[:], -0.125, col(T.CS, 0), MUL, MUL))
    e_sm = mark(V.tensor_scalar(T.SM[:], T.X3[:], 128.0, None, MUL))
    e_t2 = mark(V.tensor_scalar(T.T2[:], T.X3[:], 1.0 / 1024, 0.01, MUL, ADD))
    ws(*own_x)
    S.wait_ge(T.sem.arrx, nax)
    ws(e_ns, e_cs)
    e_q = [mark(S.activation(T.J8[:, j, :], GX[:, :, _mc(j)], ACT.Square, bias=col(T.NS, _mc(j)), scale=col(T.CS, 0),
                             accum_out=col(T.QV, _mc(j) + 1))) for j in range(n)]
    wv(e_sm)
    e_dm = [mark(V.tensor_scalar(T.DM[:, :, j], GX[:, :, _mc(j)], -1024.0, col(T.SM, _mc(j)), MUL, ADD)) for j in range(n)]
    wv(*e_dm)
    e_ox = mark(V.tensor_scalar(T.OX[:], T.DM[:, r, :], -1.0 / 1024, None, MUL))
    wv(e_t2, *e_q)
    e_ve = mark(V.tensor_tensor(T.VE[:], T.QV[:, 1:H:2], T.T2[:, 1:H:2], ADD))
    wv(e_ve)
    e_r2 = mark(V.reciprocal(T.RS2[:], T.VE[:]))
    ws(e_r2)
    e_rs = mark(S.activation(T.RS[:], T.RS2[:], ACT.Sqrt))
    wv(e_r2)
    e_n2 = mark(V.tensor_scalar(T.NR2[:], T.RS2[:], -1.0 / 1024, None, MUL))
    ws(e_rs, ci)
    e_di = [mark(S.activation(ch(T.dg, j), T.idn[:, 0:128], ACT.Copy, scale=col(T.RS, j))) for j in range(n)]

    wv(*own_d)
    V.wait_ge(T.sem.arrd, 7 * ne)
    p1 = mark(V.tensor_tensor(GD[:, 1:2 * NR:2, 0:n], T.DM[:, :, :], GD[:, 0:2 * NR:2, n:2 * n], MUL))
    ws(*own_d)
    S.wait_ge(T.sem.arrd, 7 * ne)
    ws(e_n2)
    e_be, e_dq = [], []
    for j in range(n):
        e_a = mark(S.activation(T.JA[:, j, :], GD[:, 0:2 * NR:2, n + j], ACT.Copy, accum_out=col(T.D3, n + j)))
        ws(p1)
        e_be.append(mark(S.activation(T.JB[:, j, :], GD[:, :, j], ACT.Copy, scale=col(T.NR2, j),
                                      accum_out=col(T.BE, j))))
        ws(e_a)
        e_dq.append(mark(S.activation(pd[j][:, 0:128], pd[j][:, 0:128], ACT.Identity, bias=col(T.D3, n + j))))
    wv(e_ox)

    e_st = []
    for j in range(n):
        wv(e_be[j])
        e_u = mark(V.tensor_scalar(ch(T.ub, j), ch(T.xc, j), col(T.OX, j), col(T.BE, j), ADD, MUL))
        wv(e_u, e_dq[j])
        e_v = mark(V.tensor_tensor(ch(T.vb, j), pd[j][:, 0:128], ch(T.ub, j), ADD))
        wp(e_v, e_di[j])
        if j < n - 1:
            parts = [(px[j], 0, 128)]
        else:
            parts = [(px[j], 0, 64), (pd[0], 64, 64)]
        for bank, p0, w in parts:
            c0_ = 128 * j + p0
            e_m = mark(PE.matmul(bank[:, 0:w], T.vb[p0:p0 + w, 128 * j:128 * (j + 1)], T.dg[p0:p0 + w, c0_:c0_ + w],
                                 True, True))
            ws(e_m)
            e_c = mark(S.activation(T.ob[:, c0_:c0_ + w], bank[:, 0:w], ACT.Copy))
            wy(e_c)
            e_st.append(mark(SY.dma_start(T.dx[:, c0_:c0_ + w], T.ob[:, c0_:c0_ + w]), 16))

    g.wait_ge(T.sem.sent, nsent)
    g.wait_ge(T.sem.arrx, nax)
    g.wait_ge(T.sem.arrd, 7 * ne)
    wg(*[e for e in evs if not e[3]])
    wg(*e_st)
